import numpy as np
import ml_dtypes


def mxq(x, axis, fmt="e4m3"):
    dtype, down = {"e4m3": (ml_dtypes.float8_e4m3fn, 7), "e5m2": (ml_dtypes.float8_e5m2, 14)}[fmt]
    v = np.moveaxis(np.asarray(x, np.float32).astype(ml_dtypes.bfloat16).astype(np.float64), axis, -1)
    blocks = v.reshape(v.shape[:-1] + (-1, 32))
    amax = np.abs(blocks).max(-1, keepdims=True)
    byte = np.maximum(np.where(amax > 0, np.frexp(amax)[1] - 1 + 127, 0) - down, 1)
    scale = np.exp2(byte - 127.0)
    codes = (blocks / scale).astype(np.float32).astype(dtype).astype(np.float64)
    return np.moveaxis((codes * scale).reshape(v.shape), -1, axis)


WIDE = False


def mx_kscale(k):
    if not WIDE:
        return np.ones(k)
    levels = np.array([30, -30])
    if k % 512:
        return np.exp2(np.random.permutation(np.resize(levels, k // 32))).repeat(32)
    a = np.empty((k // 512, 16))
    for p in range(k // 512):
        a[p, :8] = np.random.permutation(np.resize(levels, 8))
        for g in range(8):
            far = levels[np.abs(levels - a[p, g]) >= 10]
            a[p, g + 8] = far[np.random.randint(len(far))]
    return np.exp2(a.ravel()).repeat(32)


def f64(x):
    return np.asarray(x).astype(np.float64)


def striped(idx):
    return np.tile(np.asarray(idx).reshape(-1, 16).T, (8, 1)).astype(np.uint16)


def unstriped(offs):
    return offs[:16].T.reshape(-1).astype(np.int64)


E2M1 = np.array([0.0, 0.5, 1.0, 1.5, 2.0, 3.0, 4.0, 6.0, -0.0, -0.5, -1.0, -1.5, -2.0, -3.0, -4.0, -6.0])


def pack_weight(w, fmt):
    k, n = w.shape
    w = f64(np.asarray(w, np.float32).astype(ml_dtypes.bfloat16)).reshape(k // 32, 32, n)
    amax = np.abs(w).max(1)
    if fmt == "e4m3":
        byte = np.frexp(amax)[1] - 1 + 127 - 7
    else:
        mant, ex = np.frexp(amax / 6.0)
        byte = np.where(mant > 0.5, ex, ex - 1) + 127
    byte = np.clip(np.where(amax > 0, byte, 1), 1, 254)
    scaled = (w * np.exp2(127.0 - byte)[:, None, :]).reshape(k, n).astype(np.float32)
    by_word = np.ascontiguousarray(scaled.reshape(k // 512, 128, 4, n).transpose(0, 1, 3, 2))
    if fmt == "e4m3":
        words = by_word.astype(ml_dtypes.float8_e4m3fn).view(np.uint8)
    else:
        c = by_word.astype(ml_dtypes.float4_e2m1fn).view(np.uint8) & 0xF
        words = (c[..., 0::2] | (c[..., 1::2] << 4)).reshape(k // 512, 128, 2 * n)
    return np.ascontiguousarray(words), np.ascontiguousarray(byte.astype(np.uint8).reshape(k // 512, 16, n))


def unpack_weight(words, scales, fmt):
    g, _, n = scales.shape
    words = np.ascontiguousarray(words).reshape(g, 128, n, -1)
    if fmt == "e4m3":
        vals = words.view(ml_dtypes.float8_e4m3fn).astype(np.float64)
    else:
        nib = np.empty((g, 128, n, 4), np.uint8)
        nib[..., 0::2] = words & 0xF
        nib[..., 1::2] = words >> 4
        vals = E2M1[nib]
    vals = vals * np.repeat(np.exp2(scales.astype(np.float64) - 127.0), 8, axis=1)[..., None]
    return vals.transpose(0, 1, 3, 2).reshape(g * 512, n)


def sigmoid(v):
    return 1.0 / (1.0 + np.exp(-v))


def sgn(shape):
    return np.random.uniform(0.5, 2.0, shape) * np.where(np.random.standard_normal(shape) < 0, -1.0, 1.0)


K, T, J, R, F, Z, O, U, D, N = 512, 1024, 256, 512, 512, 1024, 128, 128, 256, 256


def setup_inputs():
    n = np.random.standard_normal
    idx = np.random.permutation(T)[:J]
    idx2 = np.random.permutation(Z)[:J]
    idx3 = np.random.permutation(J)[:O]
    idx4 = np.random.permutation(J)[:O]
    idx5 = np.random.permutation(J)[:U]
    idx6 = np.random.permutation(J)[:U]
    idx7 = np.random.permutation(T)[:D]
    fk = mx_kscale(K)
    ff = mx_kscale(F)
    fr = mx_kscale(R)
    xtp = pack_weight(n((K, T)) / fk[:, None], "e2m1")
    xop = pack_weight(n((F, Z)) / ff[:, None], "e4m3")
    wp = pack_weight(n((K, R)) * 1 / np.sqrt(K) * fk[:, None], "e4m3")
    w2p = pack_weight(n((F, R)) * 1 / np.sqrt(F) * ff[:, None], "e2m1")
    wbp = pack_weight(n((R, N)) * 1 / np.sqrt(R) / fr[:, None], "e2m1")
    wsp = pack_weight(n((K, N)) * 1 / np.sqrt(K) * fk[:, None], "e4m3")
    return {
        "xt_words": xtp[0],
        "xt_scales": xtp[1],
        "xo_words": xop[0],
        "xo_scales": xop[1],
        "w_words": wp[0],
        "w_scales": wp[1],
        "w2_words": w2p[0],
        "w2_scales": w2p[1],
        "sa": (np.random.uniform(0.5, 1.6, (R, 1)) * fr[:, None]).astype(np.float32),
        "sb": (np.random.uniform(0.5, 1.6, (R, 1)) * fr[:, None]).astype(np.float32),
        "sg": (sgn((R, 1))).astype(np.float32),
        "bg": (np.random.uniform(-2.0, 2.0, (R, 1))).astype(np.float32),
        "sh": (sgn((R, 1))).astype(np.float32),
        "bh": (np.random.uniform(-2.0, 2.0, (R, 1))).astype(np.float32),
        "wb_words": wbp[0],
        "wb_scales": wbp[1],
        "ws_words": wsp[0],
        "ws_scales": wsp[1],
        "offs": striped(idx),
        "offs2": striped(idx2),
        "offs3": striped(idx3),
        "offs4": striped(idx4),
        "offs5": striped(idx5),
        "offs6": striped(idx6),
        "offs7": striped(idx7),
    }


def reference(xt_words, xt_scales, xo_words, xo_scales, w_words, w_scales, w2_words, w2_scales, sa, sb, sg, bg, sh, bh, wb_words, wb_scales, ws_words, ws_scales, offs, offs2, offs3, offs4, offs5, offs6, offs7):
    idx = unstriped(offs)
    idx2 = unstriped(offs2)
    idx3 = unstriped(offs3)
    idx4 = unstriped(offs4)
    idx5 = unstriped(offs5)
    idx6 = unstriped(offs6)
    idx7 = unstriped(offs7)
    xtu = unpack_weight(xt_words, xt_scales, "e2m1")
    xou = unpack_weight(xo_words, xo_scales, "e4m3")
    wu = unpack_weight(w_words, w_scales, "e4m3")
    w2u = unpack_weight(w2_words, w2_scales, "e2m1")
    wbu = unpack_weight(wb_words, wb_scales, "e2m1")
    wsu = unpack_weight(ws_words, ws_scales, "e4m3")
    xtidxg = xtu[:, idx]
    a = wu.T @ xtidxg
    xoidx2g = xou[:, idx2]
    b = w2u.T @ xoidx2g
    h1 = a[:, idx3] * f64(sa) * sigmoid(a[:, idx4] * f64(sg) + f64(bg))
    h2 = b[:, idx5] * f64(sb) * sigmoid(b[:, idx6] * f64(sh) + f64(bh))
    hid = np.concatenate([h1, h2], axis=1)
    hidq = mxq(hid, 0, "e5m2")
    xtidx7g = xtu[:, idx7]
    y = wbu.T @ hidq + wsu.T @ xtidx7g
    return y

from contextlib import ExitStack

import concourse.mybir as mybir

K, T, J, R, F, Z, O, U, D, N = 512, 1024, 256, 512, 512, 1024, 128, 128, 256, 256
FLOPS = 2 * (K * R * J + F * R * J + R * N * D + K * N * D)

F32 = mybir.dt.float32
BF16 = mybir.dt.bfloat16
I32 = mybir.dt.int32
U32 = mybir.dt.uint32
U16 = mybir.dt.uint16
U8 = mybir.dt.uint8
E4M3 = mybir.dt.float8_e4m3fn_x4
E5M2 = mybir.dt.float8_e5m2_x4
E2M1 = mybir.dt.float4_e2m1fn_x4
ACT = mybir.ActivationFunctionType
MULT = mybir.AluOpType.mult

P = 128
PACK = 4
QUADS = 4


def tile_list_gatedsides_twotab_further_plain_kernel(
    tc, xt_words, xt_scales, xo_words, xo_scales, w_words, w_scales, w2_words, w2_scales,
    sa, sb, sg, bg, sh, bh, wb_words, wb_scales, ws_words, ws_scales,
    offs, offs2, offs3, offs4, offs5, offs6, offs7, out,
):
    nc = tc.nc
    with ExitStack() as ctx:
        sbuf = ctx.enter_context(tc.tile_pool(name="sbuf", bufs=1))
        ring = ctx.enter_context(tc.psum_pool(name="ring", bufs=4))
        sums = ctx.enter_context(tc.psum_pool(name="sums", bufs=1))

        def new(name, shape, dtype, tag=""):
            return sbuf.tile(shape, dtype, name=name, tag=tag, align_bytes=64)

        def load_list(name, src):
            t = sbuf.tile(list(src.shape), U16, name=name)
            nc.sync.dma_start(t[:], src)
            return t

        def load_words(queue, name, src, dtype, cols):
            t = new(name, [P, cols], dtype)
            flat = src[0] if len(src.shape) == 3 else src[0].rearrange("p c r -> p (c r)")
            queue.dma_start(t[:].bitcast(I32), flat.bitcast(I32))
            return t

        def zeroed_plane(name, cols):
            t = new(name, [P, cols], U8)
            nc.vector.memset(t[:].bitcast(I32), 0)
            return t

        def load_plane(queue, plane, src):
            for q in range(QUADS):
                queue.dma_start(plane[32 * q : 32 * q + 4, :].bitcast(I32), src[0, 4 * q : 4 * q + 4, :].bitcast(I32))

        def load_staged(queue, name, src):
            cols = src.shape[2]
            t = new(name, [4, QUADS, cols // 4], I32)
            queue.dma_start(t[:], src[0].bitcast(I32).rearrange("(q r) n -> r q n", r=4))
            return t

        def spread(plane, staged):
            for q in range(QUADS):
                nc.vector.tensor_copy(plane[32 * q : 32 * q + 4, :].bitcast(I32), staged[:, q, :])

        def load_rows(queue, name, src):
            t = new(name, [P, PACK], F32)
            queue.dma_start(t[:], src.rearrange("(p t) o -> p (t o)", t=PACK))
            return t

        def gather(name, window, offsets, dtype, n, tag=""):
            t = new(name, [P, n], dtype, tag)
            nc.vector.tensor_copy(t[:], window.indirect(offsets[:]))
            return t

        def deal(copy, name, src, dtype, run, tag=""):
            t = new(name, [P, R], dtype, tag)
            copy(
                t[:].rearrange("p (t c i) -> p c t i", t=PACK, i=run),
                src.rearrange("p (c i t) -> p c t i", t=PACK, i=run),
            )
            return t


        xt_plane = zeroed_plane("xt_plane", T)
        w_plane = zeroed_plane("w_plane", R)
        xo_plane = zeroed_plane("xo_plane", Z)
        w2_plane = zeroed_plane("w2_plane", R)
        ws_plane = zeroed_plane("ws_plane", N)
        wb_plane = zeroed_plane("wb_plane", N)

        sg_t = load_rows(nc.gpsimd, "sg_t", sg)
        bg_t = load_rows(nc.gpsimd, "bg_t", bg)
        sa_t = load_rows(nc.gpsimd, "sa_t", sa)
        list1 = load_list("list1", offs)
        w_staged = load_staged(nc.sync, "w_staged", w_scales)
        xt_w = load_words(nc.sync, "xt_w", xt_words, U16, T)
        load_plane(nc.sync, xt_plane, xt_scales)
        w_w = load_words(nc.sync, "w_w", w_words, U32, R)
        w2_w = load_words(nc.sync, "w2_w", w2_words, U16, R)
        xo_w = load_words(nc.sync, "xo_w", xo_words, U32, Z)
        list4 = load_list("list4", offs4)
        list3 = load_list("list3", offs3)
        list2 = load_list("list2", offs2)
        load_plane(nc.sync, xo_plane, xo_scales)
        w2_staged = load_staged(nc.sync, "w2_staged", w2_scales)
        list7 = load_list("list7", offs7)
        list6 = load_list("list6", offs6)
        list5 = load_list("list5", offs5)
        sh_t = load_rows(nc.sync, "sh_t", sh)
        bh_t = load_rows(nc.sync, "bh_t", bh)
        sb_t = load_rows(nc.sync, "sb_t", sb)
        ws_w = load_words(nc.sync, "ws_w", ws_words, U32, N)
        load_plane(nc.sync, ws_plane, ws_scales)
        load_plane(nc.sync, wb_plane, wb_scales)
        wb_w = load_words(nc.sync, "wb_w", wb_words, U16, N)

        def first_stage(name, w_codes, w_fmt, w_sc, x_codes, x_fmt, x_sc, movers):
            rows = []
            for t in range(PACK):
                cols = slice(P * t, P * (t + 1))
                acc = ring.tile([P, J], F32, name="acc")
                nc.tensor.matmul_mx(
                    out=acc[:], lhsT=w_codes[:, cols].bitcast(w_fmt), lhsT_scale=w_sc[:, cols],
                    rhs=x_codes[:].bitcast(x_fmt), rhs_scale=x_sc[:], start=True, stop=True,
                )
                row = new("%s%d" % (name, t), [P, J], F32)
                movers[t](row[:], acc[:])
                rows.append(row)
            return rows

        def looks(name, rows, val_list, gate_list, weight, slope, offset):
            gate = new(name + "_gate", [P, PACK, O], F32)
            val = new(name + "_val", [P, PACK, O], F32)
            for t in range(PACK):
                col = slice(t, t + 1)
                nc.scalar.activation(gate[:, t, :], rows[t][:].indirect(gate_list[:]), ACT.Sigmoid, bias=offset[:, col], scale=slope[:, col])
                nc.scalar.activation(val[:, t, :], rows[t][:].indirect(val_list[:]), ACT.Copy, scale=weight[:, col])
            return gate, val

        def hidden(name, gate, val, tag=""):
            hid = new(name + "_hid", [P, O * PACK], BF16, tag)
            nc.vector.tensor_tensor(
                hid[:].rearrange("p (c i t) -> p c t i", t=PACK, i=2),
                val[:].rearrange("p t (c i) -> p c t i", i=2),
                gate[:].rearrange("p t (c i) -> p c t i", i=2),
                MULT,
            )
            codes = new(name + "_codes", [P, O], U32)
            plane = new(name + "_plane", [P, O], U8)
            nc.vector.quantize_mx(out=codes[:].bitcast(E5M2), scales=plane[:], in_=hid[:])
            return codes, plane

        vec, sca = nc.vector.tensor_copy, nc.scalar.copy

        xt1_sc = gather("xt1_sc", xt_plane[:], list1, U8, J)
        spread(w_plane, w_staged)
        w_sc = deal(vec, "w_sc", w_plane[:], U8, 16)
        xt1_w = gather("xt1_w", xt_w[:], list1, U16, J)
        w_d = deal(sca, "w_d", w_w[:], U32, 4)
        a_rows = first_stage("a", w_d, E4M3, w_sc, xt1_w, E2M1, xt1_sc, [sca, vec, vec, vec])

        xo2_sc = gather("xo2_sc", xo_plane[:], list2, U8, J, "late_sc")
        xo2_w = gather("xo2_w", xo_w[:], list2, U32, J, "late_w")
        spread(w2_plane, w2_staged)
        w2_sc = deal(vec, "w2_sc", w2_plane[:], U8, 16)
        w2_d = deal(sca, "w2_d", w2_w[:], U16, 8, "dealt")
        gate_a, val_a = looks("a", a_rows, list3, list4, sa_t, sg_t, bg_t)
        b_rows = first_stage("b", w2_d, E2M1, w2_sc, xo2_w, E4M3, xo2_sc, [vec, vec, vec, vec])
        gate_b, val_b = looks("b", b_rows, list5, list6, sb_t, sh_t, bh_t)

        xt7_sc = gather("xt7_sc", xt_plane[:], list7, U8, D, "late_sc")
        xt7_w = gather("xt7_w", xt_w[:], list7, U16, D, "late_w")

        def short_way(dst, j, h, start):
            ncols, dcols = slice(P * j, P * (j + 1)), slice(O * h, O * (h + 1))
            nc.tensor.matmul_mx(
                out=dst, lhsT=ws_w[:, ncols].bitcast(E4M3), lhsT_scale=ws_plane[:, ncols],
                rhs=xt7_w[:, dcols].bitcast(E2M1), rhs_scale=xt7_sc[:, dcols], start=start, stop=False,
            )

        def long_way(dst, j, codes, plane, stop):
            ncols = slice(P * j, P * (j + 1))
            nc.tensor.matmul_mx(
                out=dst, lhsT=wb_w[:, ncols].bitcast(E2M1), lhsT_scale=wb_plane[:, ncols],
                rhs=codes[:].bitcast(E5M2), rhs_scale=plane[:], start=False, stop=stop,
            )

        y_a = sums.tile([P, 2, O], F32, name="y_a")
        y_b = [sums.tile([P, U], F32, name="y_b%d" % j) for j in range(2)]
        for j in range(2):
            short_way(y_a[:, j, :], j, 0, j == 0)
        for j in range(2):
            short_way(y_b[j][:], j, 1, True)

        codes_a, plane_a = hidden("a", gate_a, val_a, "dealt")
        for j in range(2):
            long_way(y_a[:, j, :], j, codes_a, plane_a, j == 1)
        res_a = new("res_a", [P, 2, O], F32)
        nc.scalar.copy(res_a[:], y_a[:])
        nc.sync.dma_start(out.rearrange("(j p) d -> p j d", p=P)[:, :, 0:O], res_a[:])

        codes_b, plane_b = hidden("b", gate_b, val_b)
        for j, (mover, queue) in enumerate(((sca, nc.scalar), (vec, nc.sync))):
            long_way(y_b[j][:], j, codes_b, plane_b, True)
            res_b = new("res_b%d" % j, [P, U], F32)
            mover(res_b[:], y_b[j][:])
            queue.dma_start(out[P * j : P * (j + 1), O:D], res_b[:])
